import numpy as np
import ml_dtypes


def mxq(x, axis, fmt="e4m3"):
    dtype, down = {"e4m3": (ml_dtypes.float8_e4m3fn, 7), "e5m2": (ml_dtypes.float8_e5m2, 14)}[fmt]
    v = np.moveaxis(np.asarray(x, np.float32).astype(ml_dtypes.bfloat16).astype(np.float64), axis, -1)
    blocks = v.reshape(v.shape[:-1] + (-1, 32))
    amax = np.abs(blocks).max(-1, keepdims=True)
    byte = np.maximum(np.where(amax > 0, np.frexp(amax)[1] - 1 + 127, 0) - down, 1)
    scale = np.exp2(byte - 127.0)
    codes = (blocks / scale).astype(np.float32).astype(dtype).astype(np.float64)
    return np.moveaxis((codes * scale).reshape(v.shape), -1, axis)


WIDE = False


def mx_kscale(k):
    if not WIDE:
        return np.ones(k)
    levels = np.array([10, -10, 5, -5, 0])
    if k % 512:
        return np.exp2(np.random.permutation(np.resize(levels, k // 32))).repeat(32)
    a = np.empty((k // 512, 16))
    for p in range(k // 512):
        a[p, :8] = np.random.permutation(np.resize(levels, 8))
        for g in range(8):
            far = levels[np.abs(levels - a[p, g]) >= 10]
            a[p, g + 8] = far[np.random.randint(len(far))]
    return np.exp2(a.ravel()).repeat(32)


def f64(x):
    return np.asarray(x).astype(np.float64)


def striped(idx):
    return np.tile(idx.reshape(-1, 16).T, (8, 1)).astype(np.uint16)


def unstriped(offs):
    return offs[:16].T.reshape(-1).astype(np.int64)


def striped8(idx):
    return np.concatenate([x.reshape(-1, 16).T for x in idx]).astype(np.uint16)


def runs(offs, k):
    lists = np.stack([offs[16 * r : 16 * r + 16].T.reshape(-1) for r in range(8)]).astype(np.int64)
    return lists[np.arange(k) % 512 // 64]


def pack_weight(w):
    k, n = w.shape
    w = f64(np.asarray(w, np.float32).astype(ml_dtypes.bfloat16)).reshape(k // 32, 32, n)
    amax = np.abs(w).max(1)
    byte = np.clip(np.where(amax > 0, np.frexp(amax)[1] - 1 + 127 - 7, 1), 1, 254)
    scaled = (w * np.exp2(127.0 - byte)[:, None, :]).reshape(k, n).astype(np.float32)
    words = np.ascontiguousarray(scaled.reshape(k // 512, 128, 4, n).transpose(0, 1, 3, 2)).astype(ml_dtypes.float8_e4m3fn).view(np.uint8)
    return words, np.ascontiguousarray(byte.astype(np.uint8).reshape(k // 512, 16, n))


def unpack_weight(words, scales):
    g, p, n, _ = words.shape
    vals = np.ascontiguousarray(words).view(ml_dtypes.float8_e4m3fn).astype(np.float64) * np.repeat(np.exp2(scales.astype(np.float64) - 127.0), 8, axis=1)[..., None]
    return vals.transpose(0, 1, 3, 2).reshape(g * 512, n)


def sigmoid(v):
    return 1.0 / (1.0 + np.exp(-np.maximum(v, -700.0)))


K, T, S, N, H = 512, 2048, 512, 512, 512


def setup_inputs():
    n = np.random.standard_normal
    s = mx_kscale(K)[:, None]
    u = mx_kscale(H)
    packed_xT = pack_weight(n((K, T)) * s)
    return {
        "x_words": packed_xT[0],
        "x_scales": packed_xT[1],
        "w1": (n((K, H)) / np.sqrt(K) / s).astype(np.float32),
        "w2": (n((K, H)) / np.sqrt(K) / s).astype(np.float32),
        "w3": (n((K, H)) / np.sqrt(K) / s).astype(np.float32),
        "gn": (np.random.uniform(0.5, 1.5, (H, 1)) * u[:, None]).astype(np.float32),
        "w4": (n((H, N)) / np.sqrt(H) / u[:, None]).astype(np.float32),
        "offs": striped(np.random.permutation(T)[:S]),
        "two": striped(np.random.permutation(T)[:S]),
        "thr": striped(np.random.permutation(T)[:S]),
        "q1": striped8(np.stack([np.random.permutation(S) for _ in range(8)])),
        "q2": striped8(np.stack([np.random.permutation(S) for _ in range(8)])),
        "q3": striped8(np.stack([np.random.permutation(S) for _ in range(8)])),
        "q4": striped8(np.stack([np.random.permutation(S) for _ in range(8)])),
    }


def reference(x_words, x_scales, w1, w2, w3, gn, w4, offs, two, thr, q1, q2, q3, q4):
    xq = unpack_weight(x_words, x_scales)[:, unstriped(offs)]
    y = mxq(f64(w1), 0, "e4m3").T @ xq
    x_two = unpack_weight(x_words, x_scales)[:, unstriped(two)]
    fx = sigmoid(mxq(f64(w2), 0, "e4m3").T @ x_two)
    top = y[np.arange(H)[:, None], runs(q1, H)] + fx * (y[np.arange(H)[:, None], runs(q2, H)] - (y[np.arange(H)[:, None], runs(q1, H)]))
    x_thr = unpack_weight(x_words, x_scales)[:, unstriped(thr)]
    fy = sigmoid(mxq(f64(w3), 0, "e4m3").T @ x_thr)
    bot = y[np.arange(H)[:, None], runs(q3, H)] + fx * (y[np.arange(H)[:, None], runs(q4, H)] - (y[np.arange(H)[:, None], runs(q3, H)]))
    z = f64(gn) * (top + fy * (bot - top))
    return mxq(f64(w4), 0, "e4m3").T @ mxq(z, 0, "e4m3")

@@ -1,0 +1,211 @@
+from contextlib import ExitStack
+
+import concourse.mybir as mybir
+from concourse.masks import make_identity
+
+K, T, S, H, N = 512, 2048, 512, 512, 512
+FLOPS = 4 * 2 * 512 * 512 * 512
+
+F32 = mybir.dt.float32
+BF16 = mybir.dt.bfloat16
+I32 = mybir.dt.int32
+U32 = mybir.dt.uint32
+U16 = mybir.dt.uint16
+U8 = mybir.dt.uint8
+FP8X4 = mybir.dt.float8_e4m3fn_x4
+ACT = mybir.ActivationFunctionType
+ALU = mybir.AluOpType
+
+P = 128
+PACK = 4
+BLK = 128
+NBLK = S // BLK
+LANES = 16
+
+
+def tile_picked_bilcomp_none_p_kernel(tc, x_words, x_scales, w1, w2, w3, gn, w4, offs, two, thr, q1, q2, q3, q4, out):
+    nc = tc.nc
+    with ExitStack() as ctx:
+        keep = ctx.enter_context(tc.tile_pool(name="keep", bufs=1))
+        ring = ctx.enter_context(tc.tile_pool(name="ring", bufs=2))
+        psum = ctx.enter_context(tc.psum_pool(name="psum", bufs=1))
+
+        def load_list(name, src):
+            tile = keep.tile([P, S // LANES], U16, name=name)
+            nc.sync.dma_start(tile[:], src)
+            return tile
+
+        def load_weight(name, w, c0, width):
+            raw = keep.tile([P, PACK, width], F32, name=name)
+            nc.sync.dma_start(raw[:], w.rearrange("(p j) c -> p j c", j=PACK)[:, :, c0 : c0 + width])
+            return raw
+
+        table_words = keep.tile([P, T], U32, name="table_words")
+        table_bytes = keep.tile([P, T], U8, name="table_bytes")
+        nc.sync.dma_start(table_words[:].bitcast(I32), x_words[0].rearrange("p c r -> p (c r)").bitcast(I32))
+        offs_sb = load_list("offs_sb", offs)
+        for q in range(4):
+            nc.sync.dma_start(table_bytes[32 * q : 32 * q + 32, :].bitcast(I32), x_scales[0, 4 * q : 4 * q + 4, :].bitcast(I32).partition_broadcast(8))
+        w1_raw = [load_weight("w1_raw%d" % h, w1, h * (H // 2), H // 2) for h in range(2)]
+        two_sb = load_list("two_sb", two)
+        gain = keep.tile([P, PACK], F32, name="gain")
+        nc.gpsimd.dma_start(gain[:], gn.rearrange("(p t) o -> p (t o)", t=PACK))
+        corner_lists = [load_list("q%d_sb" % (n + 1), q) for n, q in enumerate((q1, q2, q3, q4))]
+        w2_raw = load_weight("w2_raw", w2, 0, H)
+        thr_sb = load_list("thr_sb", thr)
+        w3_raw = load_weight("w3_raw", w3, 0, H)
+        w4_raw = load_weight("w4_raw", w4, 0, N)
+
+        ident = keep.tile([P, P], F32, name="ident")
+        make_identity(nc, ident[:])
+
+        def pick_columns(name, lst, words_tag, scale_tag):
+            words = keep.tile([P, S], U32, name=name + "_words", tag=words_tag, align_bytes=64)
+            scale = keep.tile([P, S], U8, name=name + "_scale", tag=scale_tag, align_bytes=64)
+            nc.vector.tensor_copy(words[:], table_words[:].indirect(lst[:]))
+            nc.vector.tensor_copy(scale[:], table_bytes[:].indirect(lst[:]))
+            return words, scale
+
+        def quantize(name, grouped):
+            width = grouped.shape[1] // PACK
+            codes = keep.tile([P, width], U32, name=name + "_codes", tag=name + "_codes", align_bytes=64)
+            scale = keep.tile([P, width], U8, name=name + "_qscale", tag=name + "_qscale", align_bytes=64)
+            nc.vector.quantize_mx(out=codes[:].bitcast(FP8X4), scales=scale[:], in_=grouped[:])
+            return codes, scale
+
+        def quantize_weight(name, raw):
+            codes = keep.tile([P, H], U32, name=name + "_codes", tag=name + "_codes", align_bytes=64)
+            scale = keep.tile([P, H], U8, name=name + "_qscale", tag=name + "_qscale", align_bytes=64)
+            src = raw[:].rearrange("p j c -> p c j")
+            half = H // 2
+            for u in range(2):
+                grouped = keep.tile([P, PACK * half], BF16, name="%s_grouped%d" % (name, u), tag="%s_stage%d" % (name, u), align_bytes=64)
+                dst = grouped[:].rearrange("p (c j) -> p c j", j=PACK)
+                for c in range(0, half, P):
+                    nc.gpsimd.tensor_scalar(dst[:, c : c + P], src[:, u * half + c : u * half + c + P], 1.0, 0.0, ALU.mult, ALU.add)
+                cols = slice(u * half, (u + 1) * half)
+                nc.vector.quantize_mx(out=codes[:, cols].bitcast(FP8X4), scales=scale[:, cols], in_=grouped[:])
+            return codes, scale
+
+        def mx(acc, lhs, lcols, rhs, rcols):
+            nc.tensor.matmul_mx(
+                out=acc,
+                lhsT=lhs[0][:, lcols].bitcast(FP8X4),
+                lhsT_scale=lhs[1][:, lcols],
+                rhs=rhs[0][:, rcols].bitcast(FP8X4),
+                rhs_scale=rhs[1][:, rcols],
+                start=True,
+                stop=True,
+            )
+
+        x_one = pick_columns("x_one", offs_sb, "x_one_words", "x_one_scale")
+        half_m = P // 2
+        w1_grouped = [keep.tile([P, 2 * PACK * P], BF16, name="w1_grouped%d" % u, tag="w1_stage%d" % u, align_bytes=64) for u in range(2)]
+        for h in range(2):
+            src = w1_raw[h][:].rearrange("p j (m t) -> p m t j", t=PACK)
+            for u in range(2):
+                dst = w1_grouped[u][:].rearrange("p (t m j) -> p m t j", t=2, j=PACK)[:, h * half_m : (h + 1) * half_m]
+                if h == 0:
+                    nc.scalar.copy(dst, src[:, :, 2 * u : 2 * u + 2, :])
+                else:
+                    nc.vector.tensor_copy(dst, src[:, :, 2 * u : 2 * u + 2, :])
+        w1_q = [quantize("w1_%d" % u, w1_grouped[u]) for u in range(2)]
+        y = []
+        for t in range(PACK):
+            bank = psum.tile([P, S], F32, name="y_bank%d" % t, tag="bank%d" % t)
+            mx(bank[:], w1_q[t // 2], slice((t % 2) * P, (t % 2 + 1) * P), x_one, slice(0, S))
+            y_t = keep.tile([P, S], F32, name="y%d" % t)
+            nc.scalar.activation(y_t[:], bank[:], ACT.Copy, scale=gain[:, t : t + 1])
+            y.append(y_t)
+
+        diff_banks = ((5, 4, 6), (2, 7, 3))
+        fraction_banks = (7, 3, 2, 0, 1, 0, 1, 0)
+
+        def gather_corners(b):
+            entries = slice(b * BLK // LANES, (b + 1) * BLK // LANES)
+            corners = {}
+            for tag, engine, members in corner_homes[b]:
+                home = keep.tile([P, len(members), BLK], F32, name="corners%d_%s" % (b, tag), tag=tag, align_bytes=64)
+                for place, (t, n) in enumerate(members):
+                    window = y[t][:].indirect(corner_lists[n][:, entries])
+                    sign = -1.0 if n in (1, 2) else 1.0
+                    if engine == "scalar":
+                        nc.scalar.activation(home[:, place], window, ACT.Copy, scale=sign)
+                    elif sign > 0:
+                        nc.vector.tensor_copy(home[:, place], window)
+                    else:
+                        nc.vector.tensor_scalar(home[:, place], window, sign, 0.0, ALU.mult, ALU.add)
+                    corners[t, n] = home[:, place]
+                if members == first_corner:
+                    corners["a"] = home
+            return corners
+
+        first_corner = [(t, 0) for t in range(PACK)]
+        rest = lambda ts: [(t, n) for t in ts for n in (1, 2, 3)]
+        corner_homes = (
+            (("a0", "scalar", first_corner), ("bcd0", "scalar", rest(range(4))),),
+            (("a1", "scalar", first_corner), ("w3_stage0", "vector", rest((0,))), ("w3_stage1", "vector", rest((1, 2, 3))),),
+            (("w4_stage0", "vector", first_corner), ("w1_stage0", "scalar", rest(range(4))),),
+            (("w4_stage1", "vector", first_corner), ("w2_stage1", "scalar", rest(range(4))),),
+        )
+
+        def turn_differences(b, corners):
+            banks = [psum.tile([P, PACK, P], F32, name="diff%d_%d" % (b, n), tag="bank%d" % diff_banks[b % 2][n]) for n in range(3)]
+            for t in range(PACK):
+                for bank, pair in zip(banks, ((0, 1), (0, 2), (2, 3))):
+                    for place, n in enumerate(pair):
+                        nc.tensor.matmul(bank[:, t, :], lhsT=corners[t, n], rhs=ident[:], start=(place == 0), stop=(place == 1), is_transpose=True)
+            return banks
+
+        x_two = pick_columns("x_two", two_sb, "w1_stage0", "w1_stage1")
+        first_corners = gather_corners(0)
+        first_banks = turn_differences(0, first_corners)
+        w2_q = quantize_weight("w2", w2_raw)
+        x_thr = pick_columns("x_thr", thr_sb, "x_one_words", "w2_stage1")
+        w3_q = quantize_weight("w3", w3_raw)
+        w4_q = quantize_weight("w4", w4_raw)
+
+        def fraction(name, x_picked, w_q, b, turn):
+            bank = psum.tile([P, H], F32, name="%s_bank%d" % (name, b), tag="bank%d" % fraction_banks[turn])
+            mx(bank[:], x_picked, slice(b * BLK, (b + 1) * BLK), w_q, slice(0, H))
+            frac = keep.tile([P, PACK, P], F32, name="%s%d" % (name, b), tag="%s%d" % (name, b), align_bytes=64)
+            nc.scalar.activation(frac[:], bank[:].rearrange("j (p t) -> j t p", t=PACK), ACT.Sigmoid)
+            return frac
+
+        factors = []
+        for b in range(NBLK):
+            fx = fraction("fx", x_two, w2_q, b, 2 * b)
+            fy = fraction("fy", x_thr, w3_q, b, 2 * b + 1)
+            fxy = keep.tile([P, PACK, P], F32, name="fxy%d" % b, tag="fxy%d" % b, align_bytes=64)
+            nc.gpsimd.tensor_tensor(fxy[:], fx[:], fy[:], ALU.mult)
+            fu = keep.tile([P, PACK, P], F32, name="fu%d" % b, tag="fu%d" % b, align_bytes=64)
+            nc.gpsimd.tensor_tensor(fu[:], fxy[:], fx[:], ALU.subtract)
+            factors.append((fu, fy, fxy))
+
+        out_rows = out.rearrange("(g p) j -> p g j", p=P)
+        for b in range(NBLK):
+            corners = first_corners if b == 0 else gather_corners(b)
+            banks = first_banks if b == 0 else turn_differences(b, corners)
+            fu, fy, fxy = factors[b]
+            terms = [ring.tile([P, PACK, P], F32, name="term%d" % n) for n in range(3)]
+            nc.vector.scalar_tensor_tensor(terms[1][:], banks[1][:], -1.0, fy[:], ALU.mult, ALU.mult)
+            nc.vector.tensor_tensor(terms[2][:], banks[2][:], fxy[:], ALU.mult)
+            nc.vector.tensor_tensor(terms[0][:], banks[0][:], fu[:], ALU.mult)
+            back = psum.tile([P, PACK, BLK], F32, name="back%d" % b, tag="bank1")
+            for place, n in enumerate((1, 2, 0)):
+                for t in range(PACK):
+                    nc.tensor.matmul(back[:, t, :], lhsT=terms[n][:, t, :], rhs=ident[:], start=(place == 0 and t == 0), stop=(place == 2 and t == PACK - 1), is_transpose=True)
+            z = ring.tile([P, BLK * PACK], BF16, name="z", align_bytes=64)
+            nc.vector.tensor_tensor(
+                z[:].rearrange("p (c i t) -> p c t i", i=2, t=PACK),
+                back[:].rearrange("p t (c i) -> p c t i", i=2),
+                corners["a"][:].rearrange("p t (c i) -> p c t i", i=2),
+                ALU.add,
+            )
+            z_q = quantize("z%d" % b, z)
+            acc = psum.tile([P, N // P, BLK], F32, name="acc%d" % b, tag="bank0")
+            for g in range(N // P):
+                mx(acc[:, g, :], w4_q, slice(g * P, (g + 1) * P), z_q, slice(0, BLK))
+            result = ring.tile([P, N // P, BLK], F32, name="result")
+            nc.scalar.copy(result[:], acc[:])
+            nc.sync.dma_start(out_rows[:, :, b * BLK : (b + 1) * BLK], result[:])

@@ -3,7 +3,7 @@ from contextlib import ExitStack
 import concourse.mybir as mybir
 from concourse.masks import make_identity
 
-K, T, S, H, N = 512, 2048, 512, 512, 512
+T, S, H, N = 2048, 512, 512, 512
 FLOPS = 4 * 2 * 512 * 512 * 512
 
 F32 = mybir.dt.float32
@@ -18,17 +18,33 @@ ALU = mybir.AluOpType
 
 P = 128
 PACK = 4
+HALF = H // 2
 BLK = 128
 NBLK = S // BLK
 LANES = 16
+QUAD = 32
+ALIGN = 64
+
+CORNER_SIGNS = (1.0, -1.0, -1.0, 1.0)
+DIFFERENCES = ((0, 1), (0, 2), (2, 3))
+
+DIFF_BANKS = ((4, 5, 6), (2, 3, 7))
+FX_BANK, FY_BANK = 0, 1
+BACK_BANK, OUT_BANK = 0, 1
+LAST_BACK_BANK, LAST_OUT_BANKS = 4, (5, 6)
 
 
 def tile_picked_bilcomp_none_p_kernel(tc, x_words, x_scales, w1, w2, w3, gn, w4, offs, two, thr, q1, q2, q3, q4, out):
     nc = tc.nc
     with ExitStack() as ctx:
         keep = ctx.enter_context(tc.tile_pool(name="keep", bufs=1))
-        ring = ctx.enter_context(tc.tile_pool(name="ring", bufs=2))
         psum = ctx.enter_context(tc.psum_pool(name="psum", bufs=1))
+
+        def sbuf_tile(shape, dtype, name, tag=None):
+            return keep.tile(shape, dtype, name=name, tag=tag or name, align_bytes=ALIGN)
+
+        def bank_tile(shape, name, bank):
+            return psum.tile(shape, F32, name=name, tag="bank%d" % bank)
 
         def load_list(name, src):
             tile = keep.tile([P, S // LANES], U16, name=name)
@@ -42,170 +58,190 @@ def tile_picked_bilcomp_none_p_kernel(tc, x_words, x_scales, w1, w2, w3, gn, w4,
 
         table_words = keep.tile([P, T], U32, name="table_words")
         table_bytes = keep.tile([P, T], U8, name="table_bytes")
-        nc.sync.dma_start(table_words[:].bitcast(I32), x_words[0].rearrange("p c r -> p (c r)").bitcast(I32))
         offs_sb = load_list("offs_sb", offs)
-        for q in range(4):
-            nc.sync.dma_start(table_bytes[32 * q : 32 * q + 32, :].bitcast(I32), x_scales[0, 4 * q : 4 * q + 4, :].bitcast(I32).partition_broadcast(8))
-        w1_raw = [load_weight("w1_raw%d" % h, w1, h * (H // 2), H // 2) for h in range(2)]
+        for q in range(P // QUAD):
+            rows = x_scales[0, PACK * q : PACK * (q + 1), :].bitcast(I32)
+            nc.sync.dma_start(table_bytes[QUAD * q : QUAD * (q + 1), :].bitcast(I32), rows.partition_broadcast(QUAD // PACK))
         two_sb = load_list("two_sb", two)
+        w1_raw = [load_weight("w1_raw%d" % h, w1, h * HALF, HALF) for h in range(2)]
+        thr_sb = load_list("thr_sb", thr)
+        nc.sync.dma_start(table_words[:].bitcast(I32), x_words[0].rearrange("p c r -> p (c r)").bitcast(I32))
         gain = keep.tile([P, PACK], F32, name="gain")
-        nc.gpsimd.dma_start(gain[:], gn.rearrange("(p t) o -> p (t o)", t=PACK))
+        nc.sync.dma_start(gain[:], gn.rearrange("(p t) o -> p (t o)", t=PACK))
         corner_lists = [load_list("q%d_sb" % (n + 1), q) for n, q in enumerate((q1, q2, q3, q4))]
         w2_raw = load_weight("w2_raw", w2, 0, H)
-        thr_sb = load_list("thr_sb", thr)
         w3_raw = load_weight("w3_raw", w3, 0, H)
         w4_raw = load_weight("w4_raw", w4, 0, N)
 
         ident = keep.tile([P, P], F32, name="ident")
         make_identity(nc, ident[:])
 
-        def pick_columns(name, lst, words_tag, scale_tag):
-            words = keep.tile([P, S], U32, name=name + "_words", tag=words_tag, align_bytes=64)
-            scale = keep.tile([P, S], U8, name=name + "_scale", tag=scale_tag, align_bytes=64)
-            nc.vector.tensor_copy(words[:], table_words[:].indirect(lst[:]))
+        def pick_scales(name, lst):
+            scale = sbuf_tile([P, S], U8, name + "_scale")
             nc.vector.tensor_copy(scale[:], table_bytes[:].indirect(lst[:]))
-            return words, scale
+            return scale
+
+        def pick_words(name, lst, tag):
+            words = sbuf_tile([P, S], U32, name + "_words", tag)
+            nc.vector.tensor_copy(words[:], table_words[:].indirect(lst[:]))
+            return words
 
         def quantize(name, grouped):
             width = grouped.shape[1] // PACK
-            codes = keep.tile([P, width], U32, name=name + "_codes", tag=name + "_codes", align_bytes=64)
-            scale = keep.tile([P, width], U8, name=name + "_qscale", tag=name + "_qscale", align_bytes=64)
+            codes = sbuf_tile([P, width], U32, name + "_codes")
+            scale = sbuf_tile([P, width], U8, name + "_qscale")
             nc.vector.quantize_mx(out=codes[:].bitcast(FP8X4), scales=scale[:], in_=grouped[:])
             return codes, scale
 
-        def quantize_weight(name, raw):
-            codes = keep.tile([P, H], U32, name=name + "_codes", tag=name + "_codes", align_bytes=64)
-            scale = keep.tile([P, H], U8, name=name + "_qscale", tag=name + "_qscale", align_bytes=64)
-            src = raw[:].rearrange("p j c -> p c j")
-            half = H // 2
+        def quantize_weight(name, raw, dealt):
+            codes = sbuf_tile([P, H], U32, name + "_codes")
+            scale = sbuf_tile([P, H], U8, name + "_qscale")
+            grouped = [sbuf_tile([P, PACK * HALF], BF16, "%s_grouped%d" % (name, u), "%s_stage%d" % (name, u)) for u in range(2)]
             for u in range(2):
-                grouped = keep.tile([P, PACK * half], BF16, name="%s_grouped%d" % (name, u), tag="%s_stage%d" % (name, u), align_bytes=64)
-                dst = grouped[:].rearrange("p (c j) -> p c j", j=PACK)
-                for c in range(0, half, P):
-                    nc.gpsimd.tensor_scalar(dst[:, c : c + P], src[:, u * half + c : u * half + c + P], 1.0, 0.0, ALU.mult, ALU.add)
-                cols = slice(u * half, (u + 1) * half)
-                nc.vector.quantize_mx(out=codes[:, cols].bitcast(FP8X4), scales=scale[:, cols], in_=grouped[:])
+                if dealt:
+                    src = raw[:].rearrange("p j (m t) -> p m t j", t=PACK)[:, :, 2 * u : 2 * u + 2, :]
+                    dst = grouped[u][:].rearrange("p (t m j) -> p m t j", t=2, j=PACK)
+                else:
+                    src = raw[:, :, u * HALF : (u + 1) * HALF].rearrange("p j (c i) -> p c j i", i=4)
+                    dst = grouped[u][:].rearrange("p (c i j) -> p c j i", i=4, j=PACK)
+                nc.vector.tensor_copy(dst, src)
+            for u in range(2):
+                cols = slice(u * HALF, (u + 1) * HALF)
+                nc.vector.quantize_mx(out=codes[:, cols].bitcast(FP8X4), scales=scale[:, cols], in_=grouped[u][:])
             return codes, scale
 
-        def mx(acc, lhs, lcols, rhs, rcols):
+        def product(acc, stationary, stationary_cols, moving, moving_cols):
             nc.tensor.matmul_mx(
                 out=acc,
-                lhsT=lhs[0][:, lcols].bitcast(FP8X4),
-                lhsT_scale=lhs[1][:, lcols],
-                rhs=rhs[0][:, rcols].bitcast(FP8X4),
-                rhs_scale=rhs[1][:, rcols],
+                lhsT=stationary[0][:, stationary_cols].bitcast(FP8X4),
+                lhsT_scale=stationary[1][:, stationary_cols],
+                rhs=moving[0][:, moving_cols].bitcast(FP8X4),
+                rhs_scale=moving[1][:, moving_cols],
                 start=True,
                 stop=True,
             )
 
-        x_one = pick_columns("x_one", offs_sb, "x_one_words", "x_one_scale")
-        half_m = P // 2
-        w1_grouped = [keep.tile([P, 2 * PACK * P], BF16, name="w1_grouped%d" % u, tag="w1_stage%d" % u, align_bytes=64) for u in range(2)]
+        def turn(acc, tile, start, stop):
+            nc.tensor.matmul(acc, lhsT=tile, rhs=ident[:], start=start, stop=stop, is_transpose=True)
+
+        scale_one, scale_two, scale_thr = [pick_scales(name, lst) for name, lst in (("x_one", offs_sb), ("x_two", two_sb), ("x_thr", thr_sb))]
+
+        w1_grouped = [sbuf_tile([P, 2 * PACK * P], BF16, "w1_grouped%d" % u, "w1_stage%d" % u) for u in range(2)]
         for h in range(2):
             src = w1_raw[h][:].rearrange("p j (m t) -> p m t j", t=PACK)
             for u in range(2):
-                dst = w1_grouped[u][:].rearrange("p (t m j) -> p m t j", t=2, j=PACK)[:, h * half_m : (h + 1) * half_m]
-                if h == 0:
-                    nc.scalar.copy(dst, src[:, :, 2 * u : 2 * u + 2, :])
-                else:
-                    nc.vector.tensor_copy(dst, src[:, :, 2 * u : 2 * u + 2, :])
+                dst = w1_grouped[u][:].rearrange("p (t m j) -> p m t j", t=2, j=PACK)[:, h * (P // 2) : (h + 1) * (P // 2)]
+                nc.scalar.copy(dst, src[:, :, 2 * u : 2 * u + 2, :])
         w1_q = [quantize("w1_%d" % u, w1_grouped[u]) for u in range(2)]
+        x_one = (pick_words("x_one", offs_sb, None), scale_one)
+
         y = []
         for t in range(PACK):
-            bank = psum.tile([P, S], F32, name="y_bank%d" % t, tag="bank%d" % t)
-            mx(bank[:], w1_q[t // 2], slice((t % 2) * P, (t % 2 + 1) * P), x_one, slice(0, S))
+            bank = bank_tile([P, S], "y_bank%d" % t, t)
+            product(bank[:], w1_q[t // 2], slice((t % 2) * P, (t % 2 + 1) * P), x_one, slice(0, S))
             y_t = keep.tile([P, S], F32, name="y%d" % t)
             nc.scalar.activation(y_t[:], bank[:], ACT.Copy, scale=gain[:, t : t + 1])
             y.append(y_t)
 
-        diff_banks = ((5, 4, 6), (2, 7, 3))
-        fraction_banks = (7, 3, 2, 0, 1, 0, 1, 0)
+        corner_a = [(t, 0) for t in range(PACK)]
 
-        def gather_corners(b):
+        def other_corners(tiles):
+            return [(t, n) for t in tiles for n in (1, 2, 3)]
+
+        fetch_plan = (
+            (("scalar", None, corner_a + other_corners(range(PACK))),),
+            (("vector", "w3_stage1", corner_a + other_corners((0, 1))), ("scalar", None, other_corners((2, 3))),),
+            (("vector", "f_ab0", corner_a), ("scalar", "w1_stage1", other_corners(range(PACK))),),
+            (("scalar", "w2_stage1", [(t, n) for n in range(4) for t in range(PACK)]),),
+        )
+        first_corner, differences, terms, z_q = {}, {}, {}, {}
+
+        def fetch(b):
             entries = slice(b * BLK // LANES, (b + 1) * BLK // LANES)
             corners = {}
-            for tag, engine, members in corner_homes[b]:
-                home = keep.tile([P, len(members), BLK], F32, name="corners%d_%s" % (b, tag), tag=tag, align_bytes=64)
+            for part, (engine, tag, members) in enumerate(fetch_plan[b]):
+                home = sbuf_tile([P, len(members), BLK], F32, "corners%d_%d" % (b, part), tag)
                 for place, (t, n) in enumerate(members):
                     window = y[t][:].indirect(corner_lists[n][:, entries])
-                    sign = -1.0 if n in (1, 2) else 1.0
                     if engine == "scalar":
-                        nc.scalar.activation(home[:, place], window, ACT.Copy, scale=sign)
-                    elif sign > 0:
+                        nc.scalar.activation(home[:, place], window, ACT.Copy, scale=CORNER_SIGNS[n])
+                    elif CORNER_SIGNS[n] > 0:
                         nc.vector.tensor_copy(home[:, place], window)
                     else:
-                        nc.vector.tensor_scalar(home[:, place], window, sign, 0.0, ALU.mult, ALU.add)
+                        nc.vector.tensor_scalar(home[:, place], window, CORNER_SIGNS[n], 0.0, ALU.mult, ALU.add)
                     corners[t, n] = home[:, place]
-                if members == first_corner:
-                    corners["a"] = home
-            return corners
-
-        first_corner = [(t, 0) for t in range(PACK)]
-        rest = lambda ts: [(t, n) for t in ts for n in (1, 2, 3)]
-        corner_homes = (
-            (("a0", "scalar", first_corner), ("bcd0", "scalar", rest(range(4))),),
-            (("a1", "scalar", first_corner), ("w3_stage0", "vector", rest((0,))), ("w3_stage1", "vector", rest((1, 2, 3))),),
-            (("w4_stage0", "vector", first_corner), ("w1_stage0", "scalar", rest(range(4))),),
-            (("w4_stage1", "vector", first_corner), ("w2_stage1", "scalar", rest(range(4))),),
-        )
-
-        def turn_differences(b, corners):
-            banks = [psum.tile([P, PACK, P], F32, name="diff%d_%d" % (b, n), tag="bank%d" % diff_banks[b % 2][n]) for n in range(3)]
+                if part == 0:
+                    first_corner[b] = home[:, 0:PACK]
+            differences[b] = [bank_tile([P, PACK, P], "diff%d_%d" % (b, n), DIFF_BANKS[b % 2][n]) for n in range(3)]
             for t in range(PACK):
-                for bank, pair in zip(banks, ((0, 1), (0, 2), (2, 3))):
-                    for place, n in enumerate(pair):
-                        nc.tensor.matmul(bank[:, t, :], lhsT=corners[t, n], rhs=ident[:], start=(place == 0), stop=(place == 1), is_transpose=True)
-            return banks
+                for bank, (first, second) in zip(differences[b], DIFFERENCES):
+                    turn(bank[:, t, :], corners[t, first], True, False)
+                    turn(bank[:, t, :], corners[t, second], False, True)
 
-        x_two = pick_columns("x_two", two_sb, "w1_stage0", "w1_stage1")
-        first_corners = gather_corners(0)
-        first_banks = turn_differences(0, first_corners)
-        w2_q = quantize_weight("w2", w2_raw)
-        x_thr = pick_columns("x_thr", thr_sb, "x_one_words", "w2_stage1")
-        w3_q = quantize_weight("w3", w3_raw)
-        w4_q = quantize_weight("w4", w4_raw)
+        x_two = (pick_words("x_two", two_sb, "w1_stage1"), scale_two)
+        w2_q = quantize_weight("w2", w2_raw, True)
+        fetch(0)
+        x_thr = (pick_words("x_thr", thr_sb, "w2_stage1"), scale_thr)
+        w3_q = quantize_weight("w3", w3_raw, True)
 
-        def fraction(name, x_picked, w_q, b, turn):
-            bank = psum.tile([P, H], F32, name="%s_bank%d" % (name, b), tag="bank%d" % fraction_banks[turn])
-            mx(bank[:], x_picked, slice(b * BLK, (b + 1) * BLK), w_q, slice(0, H))
-            frac = keep.tile([P, PACK, P], F32, name="%s%d" % (name, b), tag="%s%d" % (name, b), align_bytes=64)
-            nc.scalar.activation(frac[:], bank[:].rearrange("j (p t) -> j t p", t=PACK), ACT.Sigmoid)
+        def fraction(name, x_picked, w_q, b, bank_number):
+            bank = bank_tile([P, PACK, P], "%s_bank%d" % (name, b), bank_number)
+            product(bank[:].rearrange("j t p -> j (t p)"), x_picked, slice(b * BLK, (b + 1) * BLK), w_q, slice(0, H))
+            frac = sbuf_tile([P, PACK, P], F32, "%s%d" % (name, b))
+            nc.scalar.activation(frac[:], bank[:], ACT.Sigmoid)
             return frac
 
-        factors = []
-        for b in range(NBLK):
-            fx = fraction("fx", x_two, w2_q, b, 2 * b)
-            fy = fraction("fy", x_thr, w3_q, b, 2 * b + 1)
-            fxy = keep.tile([P, PACK, P], F32, name="fxy%d" % b, tag="fxy%d" % b, align_bytes=64)
-            nc.gpsimd.tensor_tensor(fxy[:], fx[:], fy[:], ALU.mult)
-            fu = keep.tile([P, PACK, P], F32, name="fu%d" % b, tag="fu%d" % b, align_bytes=64)
-            nc.gpsimd.tensor_tensor(fu[:], fxy[:], fx[:], ALU.subtract)
-            factors.append((fu, fy, fxy))
+        fractions = [(fraction("fx", x_two, w2_q, b, (7, 0, 1, 2, 3, 7, 0, 1)[2 * b]), fraction("fy", x_thr, w3_q, b, (7, 0, 1, 2, 3, 7, 0, 1)[2 * b + 1])) for b in range(NBLK)]
 
-        out_rows = out.rearrange("(g p) j -> p g j", p=P)
-        for b in range(NBLK):
-            corners = first_corners if b == 0 else gather_corners(b)
-            banks = first_banks if b == 0 else turn_differences(b, corners)
-            fu, fy, fxy = factors[b]
-            terms = [ring.tile([P, PACK, P], F32, name="term%d" % n) for n in range(3)]
-            nc.vector.scalar_tensor_tensor(terms[1][:], banks[1][:], -1.0, fy[:], ALU.mult, ALU.mult)
-            nc.vector.tensor_tensor(terms[2][:], banks[2][:], fxy[:], ALU.mult)
-            nc.vector.tensor_tensor(terms[0][:], banks[0][:], fu[:], ALU.mult)
-            back = psum.tile([P, PACK, BLK], F32, name="back%d" % b, tag="bank1")
-            for place, n in enumerate((1, 2, 0)):
+        def weigh(b):
+            fx, fy = fractions[b]
+            a_b, a_c, d_c = differences[b]
+            f_dc = sbuf_tile([P, PACK, P], F32, "f_dc%d" % b)
+            nc.vector.tensor_tensor(f_dc[:], fx[:], fy[:], ALU.mult)
+            f_ab = sbuf_tile([P, PACK, P], F32, "f_ab%d" % b)
+            nc.vector.scalar_tensor_tensor(f_ab[:], fy[:], 1.0, fx[:], ALU.subtract, ALU.mult)
+            terms[b] = [sbuf_tile([P, PACK, P], F32, "term%d_%d" % (b, n)) for n in range(3)]
+            nc.vector.tensor_tensor(terms[b][0][:], a_b[:], f_ab[:], ALU.mult)
+            nc.vector.scalar_tensor_tensor(terms[b][1][:], a_c[:], -1.0, fy[:], ALU.mult, ALU.mult)
+            nc.vector.tensor_tensor(terms[b][2][:], d_c[:], f_dc[:], ALU.mult)
+
+        def finish(b):
+            back = bank_tile([P, PACK, BLK], "back%d" % b, LAST_BACK_BANK if b == NBLK - 1 else BACK_BANK)
+            for n, term in enumerate(terms[b]):
                 for t in range(PACK):
-                    nc.tensor.matmul(back[:, t, :], lhsT=terms[n][:, t, :], rhs=ident[:], start=(place == 0 and t == 0), stop=(place == 2 and t == PACK - 1), is_transpose=True)
-            z = ring.tile([P, BLK * PACK], BF16, name="z", align_bytes=64)
+                    turn(back[:, t, :], term[:, t, :], n == 0 and t == 0, n == len(terms[b]) - 1 and t == PACK - 1)
+            z = sbuf_tile([P, BLK * PACK], BF16, "z%d" % b)
             nc.vector.tensor_tensor(
                 z[:].rearrange("p (c i t) -> p c t i", i=2, t=PACK),
                 back[:].rearrange("p t (c i) -> p c t i", i=2),
-                corners["a"][:].rearrange("p t (c i) -> p c t i", i=2),
+                first_corner[b].rearrange("p t (c i) -> p c t i", i=2),
                 ALU.add,
             )
-            z_q = quantize("z%d" % b, z)
-            acc = psum.tile([P, N // P, BLK], F32, name="acc%d" % b, tag="bank0")
-            for g in range(N // P):
-                mx(acc[:, g, :], w4_q, slice(g * P, (g + 1) * P), z_q, slice(0, BLK))
-            result = ring.tile([P, N // P, BLK], F32, name="result")
-            nc.scalar.copy(result[:], acc[:])
-            nc.sync.dma_start(out_rows[:, :, b * BLK : (b + 1) * BLK], result[:])
+            z_q[b] = quantize("z%d" % b, z)
+
+        out_rows = out.rearrange("(g p) j -> p g j", p=P)
+        groups = N // P
+
+        def project(b):
+            if b == NBLK - 1:
+                parts = ((0, groups // 2, LAST_OUT_BANKS[0], nc.scalar.copy), (groups // 2, groups // 2, LAST_OUT_BANKS[1], nc.vector.tensor_copy))
+            else:
+                parts = ((0, groups, OUT_BANK, nc.scalar.copy),)
+            for g0, count, bank_number, copy in parts:
+                acc = bank_tile([P, count, BLK], "acc%d_%d" % (b, g0), bank_number)
+                for g in range(count):
+                    product(acc[:, g, :], w4_q, slice((g0 + g) * P, (g0 + g + 1) * P), z_q[b], slice(0, BLK))
+                result = keep.tile([P, count, BLK], F32, name="result%d_%d" % (b, g0))
+                copy(result[:], acc[:])
+                nc.sync.dma_start(out_rows[:, g0 : g0 + count, b * BLK : (b + 1) * BLK], result[:])
+
+        for b in range(NBLK):
+            if b + 1 < NBLK:
+                fetch(b + 1)
+            weigh(b)
+            if b == 0:
+                w4_q = quantize_weight("w4", w4_raw, False)
+            finish(b)
+            if b > 0:
+                project(b - 1)
+        project(NBLK - 1)

@@ -76,6 +76,10 @@ def tile_picked_bilcomp_none_p_kernel(tc, x_words, x_scales, w1, w2, w3, gn, w4,
         ident = keep.tile([P, P], F32, name="ident")
         make_identity(nc, ident[:])
 
+        warm_up = keep.tile([P, 2], F32, name="warm_up")
+        nc.vector.memset(warm_up[:, 0:1], 0.0)
+        nc.scalar.activation(warm_up[:, 1:2], warm_up[:, 0:1], ACT.Sigmoid)
+
         def pick_scales(name, lst):
             scale = sbuf_tile([P, S], U8, name + "_scale")
             nc.vector.tensor_copy(scale[:], table_bytes[:].indirect(lst[:]))

@@ -29,7 +29,7 @@ CORNER_SIGNS = (1.0, -1.0, -1.0, 1.0)
 DIFFERENCES = ((0, 1), (0, 2), (2, 3))
 
 DIFF_BANKS = ((4, 5, 6), (2, 3, 7))
-FX_BANK, FY_BANK = 0, 1
+FRACTION_BANKS = (7, 0, 1, 2, 3)
 BACK_BANK, OUT_BANK = 0, 1
 LAST_BACK_BANK, LAST_OUT_BANKS = 4, (5, 6)
 
@@ -154,8 +154,8 @@ def tile_picked_bilcomp_none_p_kernel(tc, x_words, x_scales, w1, w2, w3, gn, w4,
 
         fetch_plan = (
             (("scalar", None, corner_a + other_corners(range(PACK))),),
-            (("vector", "w3_stage1", corner_a + other_corners((0, 1))), ("scalar", None, other_corners((2, 3))),),
-            (("vector", "f_ab0", corner_a), ("scalar", "w1_stage1", other_corners(range(PACK))),),
+            (("vector", "w3_stage1", corner_a + other_corners((0, 1, 2))), ("scalar", None, other_corners((3,)))),
+            (("vector", "w4_stage0", corner_a), ("scalar", "w1_stage1", other_corners(range(PACK)))),
             (("scalar", "w2_stage1", [(t, n) for n in range(4) for t in range(PACK)]),),
         )
         first_corner, differences, terms, z_q = {}, {}, {}, {}
@@ -187,22 +187,23 @@ def tile_picked_bilcomp_none_p_kernel(tc, x_words, x_scales, w1, w2, w3, gn, w4,
         fetch(0)
         x_thr = (pick_words("x_thr", thr_sb, "w2_stage1"), scale_thr)
         w3_q = quantize_weight("w3", w3_raw, True)
+        w4_q = quantize_weight("w4", w4_raw, False)
 
-        def fraction(name, x_picked, w_q, b, bank_number):
-            bank = bank_tile([P, PACK, P], "%s_bank%d" % (name, b), bank_number)
+        def fraction(name, x_picked, w_q, b, count):
+            bank = bank_tile([P, PACK, P], "%s_bank%d" % (name, b), FRACTION_BANKS[count % len(FRACTION_BANKS)])
             product(bank[:].rearrange("j t p -> j (t p)"), x_picked, slice(b * BLK, (b + 1) * BLK), w_q, slice(0, H))
             frac = sbuf_tile([P, PACK, P], F32, "%s%d" % (name, b))
             nc.scalar.activation(frac[:], bank[:], ACT.Sigmoid)
             return frac
 
-        fractions = [(fraction("fx", x_two, w2_q, b, (7, 0, 1, 2, 3, 7, 0, 1)[2 * b]), fraction("fy", x_thr, w3_q, b, (7, 0, 1, 2, 3, 7, 0, 1)[2 * b + 1])) for b in range(NBLK)]
+        fractions = [(fraction("fx", x_two, w2_q, b, 2 * b), fraction("fy", x_thr, w3_q, b, 2 * b + 1)) for b in range(NBLK)]
 
         def weigh(b):
             fx, fy = fractions[b]
             a_b, a_c, d_c = differences[b]
-            f_dc = sbuf_tile([P, PACK, P], F32, "f_dc%d" % b)
+            f_dc = sbuf_tile([P, PACK, P], F32, "f_dc%d" % b, "w4_stage1" if b == 0 else None)
             nc.vector.tensor_tensor(f_dc[:], fx[:], fy[:], ALU.mult)
-            f_ab = sbuf_tile([P, PACK, P], F32, "f_ab%d" % b)
+            f_ab = sbuf_tile([P, PACK, P], F32, "f_ab%d" % b, "w4_stage0" if b == 0 else None)
             nc.vector.scalar_tensor_tensor(f_ab[:], fy[:], 1.0, fx[:], ALU.subtract, ALU.mult)
             terms[b] = [sbuf_tile([P, PACK, P], F32, "term%d_%d" % (b, n)) for n in range(3)]
             nc.vector.tensor_tensor(terms[b][0][:], a_b[:], f_ab[:], ALU.mult)
@@ -231,20 +232,18 @@ def tile_picked_bilcomp_none_p_kernel(tc, x_words, x_scales, w1, w2, w3, gn, w4,
                 parts = ((0, groups // 2, LAST_OUT_BANKS[0], nc.scalar.copy), (groups // 2, groups // 2, LAST_OUT_BANKS[1], nc.vector.tensor_copy))
             else:
                 parts = ((0, groups, OUT_BANK, nc.scalar.copy),)
-            for g0, count, bank_number, copy in parts:
-                acc = bank_tile([P, count, BLK], "acc%d_%d" % (b, g0), bank_number)
-                for g in range(count):
+            for g0, width, bank_number, copy in parts:
+                acc = bank_tile([P, width, BLK], "acc%d_%d" % (b, g0), bank_number)
+                for g in range(width):
                     product(acc[:, g, :], w4_q, slice((g0 + g) * P, (g0 + g + 1) * P), z_q[b], slice(0, BLK))
-                result = keep.tile([P, count, BLK], F32, name="result%d_%d" % (b, g0))
+                result = keep.tile([P, width, BLK], F32, name="result%d_%d" % (b, g0))
                 copy(result[:], acc[:])
-                nc.sync.dma_start(out_rows[:, g0 : g0 + count, b * BLK : (b + 1) * BLK], result[:])
+                nc.sync.dma_start(out_rows[:, g0 : g0 + width, b * BLK : (b + 1) * BLK], result[:])
 
         for b in range(NBLK):
             if b + 1 < NBLK:
                 fetch(b + 1)
             weigh(b)
-            if b == 0:
-                w4_q = quantize_weight("w4", w4_raw, False)
             finish(b)
             if b > 0:
                 project(b - 1)

from contextlib import ExitStack

import concourse.mybir as mybir
from concourse.masks import make_identity

T, S, H, N = 2048, 512, 512, 512
FLOPS = 4 * 2 * 512 * 512 * 512

F32 = mybir.dt.float32
BF16 = mybir.dt.bfloat16
I32 = mybir.dt.int32
U32 = mybir.dt.uint32
U16 = mybir.dt.uint16
U8 = mybir.dt.uint8
FP8X4 = mybir.dt.float8_e4m3fn_x4
ACT = mybir.ActivationFunctionType
ALU = mybir.AluOpType

P = 128
PACK = 4
HALF = H // 2
BLK = 128
NBLK = S // BLK
LANES = 16
QUAD = 32
ALIGN = 64

CORNER_SIGNS = (1.0, -1.0, -1.0, 1.0)
DIFFERENCES = ((0, 1), (0, 2), (2, 3))

DIFF_BANKS = ((4, 5, 6), (2, 3, 7))
FRACTION_BANKS = (7, 0, 1, 2, 3)
BACK_BANK, OUT_BANK = 0, 1
LAST_BACK_BANK, LAST_OUT_BANKS = 4, (5, 6)


def tile_picked_bilcomp_none_p_kernel(tc, x_words, x_scales, w1, w2, w3, gn, w4, offs, two, thr, q1, q2, q3, q4, out):
    nc = tc.nc
    with ExitStack() as ctx:
        keep = ctx.enter_context(tc.tile_pool(name="keep", bufs=1))
        psum = ctx.enter_context(tc.psum_pool(name="psum", bufs=1))

        def sbuf_tile(shape, dtype, name, tag=None):
            return keep.tile(shape, dtype, name=name, tag=tag or name, align_bytes=ALIGN)

        def bank_tile(shape, name, bank):
            return psum.tile(shape, F32, name=name, tag="bank%d" % bank)

        def load_list(name, src):
            tile = keep.tile([P, S // LANES], U16, name=name)
            nc.sync.dma_start(tile[:], src)
            return tile

        def load_weight(name, w, c0, width):
            raw = keep.tile([P, PACK, width], F32, name=name)
            nc.sync.dma_start(raw[:], w.rearrange("(p j) c -> p j c", j=PACK)[:, :, c0 : c0 + width])
            return raw

        table_words = keep.tile([P, T], U32, name="table_words")
        table_bytes = keep.tile([P, T], U8, name="table_bytes")
        offs_sb = load_list("offs_sb", offs)
        for q in range(P // QUAD):
            rows = x_scales[0, PACK * q : PACK * (q + 1), :].bitcast(I32)
            nc.sync.dma_start(table_bytes[QUAD * q : QUAD * (q + 1), :].bitcast(I32), rows.partition_broadcast(QUAD // PACK))
        two_sb = load_list("two_sb", two)
        w1_raw = [load_weight("w1_raw%d" % h, w1, h * HALF, HALF) for h in range(2)]
        thr_sb = load_list("thr_sb", thr)
        nc.sync.dma_start(table_words[:].bitcast(I32), x_words[0].rearrange("p c r -> p (c r)").bitcast(I32))
        gain = keep.tile([P, PACK], F32, name="gain")
        nc.sync.dma_start(gain[:], gn.rearrange("(p t) o -> p (t o)", t=PACK))
        corner_lists = [load_list("q%d_sb" % (n + 1), q) for n, q in enumerate((q1, q2, q3, q4))]
        w2_raw = load_weight("w2_raw", w2, 0, H)
        w3_raw = load_weight("w3_raw", w3, 0, H)
        w4_raw = load_weight("w4_raw", w4, 0, N)

        ident = keep.tile([P, P], F32, name="ident")
        make_identity(nc, ident[:])

        warm_up = keep.tile([P, 2], F32, name="warm_up")
        nc.vector.memset(warm_up[:, 0:1], 0.0)
        nc.scalar.activation(warm_up[:, 1:2], warm_up[:, 0:1], ACT.Sigmoid)

        def pick_scales(name, lst):
            scale = sbuf_tile([P, S], U8, name + "_scale")
            nc.vector.tensor_copy(scale[:], table_bytes[:].indirect(lst[:]))
            return scale

        def pick_words(name, lst, tag):
            words = sbuf_tile([P, S], U32, name + "_words", tag)
            nc.vector.tensor_copy(words[:], table_words[:].indirect(lst[:]))
            return words

        def quantize(name, grouped):
            width = grouped.shape[1] // PACK
            codes = sbuf_tile([P, width], U32, name + "_codes")
            scale = sbuf_tile([P, width], U8, name + "_qscale")
            nc.vector.quantize_mx(out=codes[:].bitcast(FP8X4), scales=scale[:], in_=grouped[:])
            return codes, scale

        def quantize_weight(name, raw, dealt):
            codes = sbuf_tile([P, H], U32, name + "_codes")
            scale = sbuf_tile([P, H], U8, name + "_qscale")
            grouped = [sbuf_tile([P, PACK * HALF], BF16, "%s_grouped%d" % (name, u), "%s_stage%d" % (name, u)) for u in range(2)]
            for u in range(2):
                if dealt:
                    src = raw[:].rearrange("p j (m t) -> p m t j", t=PACK)[:, :, 2 * u : 2 * u + 2, :]
                    dst = grouped[u][:].rearrange("p (t m j) -> p m t j", t=2, j=PACK)
                else:
                    src = raw[:, :, u * HALF : (u + 1) * HALF].rearrange("p j (c i) -> p c j i", i=4)
                    dst = grouped[u][:].rearrange("p (c i j) -> p c j i", i=4, j=PACK)
                nc.vector.tensor_copy(dst, src)
            for u in range(2):
                cols = slice(u * HALF, (u + 1) * HALF)
                nc.vector.quantize_mx(out=codes[:, cols].bitcast(FP8X4), scales=scale[:, cols], in_=grouped[u][:])
            return codes, scale

        def product(acc, stationary, stationary_cols, moving, moving_cols):
            nc.tensor.matmul_mx(
                out=acc,
                lhsT=stationary[0][:, stationary_cols].bitcast(FP8X4),
                lhsT_scale=stationary[1][:, stationary_cols],
                rhs=moving[0][:, moving_cols].bitcast(FP8X4),
                rhs_scale=moving[1][:, moving_cols],
                start=True,
                stop=True,
            )

        def turn(acc, tile, start, stop):
            nc.tensor.matmul(acc, lhsT=tile, rhs=ident[:], start=start, stop=stop, is_transpose=True)

        scale_one, scale_two, scale_thr = [pick_scales(name, lst) for name, lst in (("x_one", offs_sb), ("x_two", two_sb), ("x_thr", thr_sb))]

        w1_grouped = [sbuf_tile([P, 2 * PACK * P], BF16, "w1_grouped%d" % u, "w1_stage%d" % u) for u in range(2)]
        for h in range(2):
            src = w1_raw[h][:].rearrange("p j (m t) -> p m t j", t=PACK)
            for u in range(2):
                dst = w1_grouped[u][:].rearrange("p (t m j) -> p m t j", t=2, j=PACK)[:, h * (P // 2) : (h + 1) * (P // 2)]
                nc.scalar.copy(dst, src[:, :, 2 * u : 2 * u + 2, :])
        w1_q = [quantize("w1_%d" % u, w1_grouped[u]) for u in range(2)]
        x_one = (pick_words("x_one", offs_sb, None), scale_one)

        y = []
        for t in range(PACK):
            bank = bank_tile([P, S], "y_bank%d" % t, t)
            product(bank[:], w1_q[t // 2], slice((t % 2) * P, (t % 2 + 1) * P), x_one, slice(0, S))
            y_t = keep.tile([P, S], F32, name="y%d" % t)
            nc.scalar.activation(y_t[:], bank[:], ACT.Copy, scale=gain[:, t : t + 1])
            y.append(y_t)

        corner_a = [(t, 0) for t in range(PACK)]

        def other_corners(tiles):
            return [(t, n) for t in tiles for n in (1, 2, 3)]

        fetch_plan = (
            (("scalar", None, corner_a + other_corners(range(PACK))),),
            (("vector", "w3_stage1", corner_a + other_corners((0, 1, 2))), ("scalar", None, other_corners((3,)))),
            (("vector", "w4_stage0", corner_a), ("scalar", "w1_stage1", other_corners(range(PACK)))),
            (("scalar", "w2_stage1", [(t, n) for n in range(4) for t in range(PACK)]),),
        )
        first_corner, differences, terms, z_q = {}, {}, {}, {}

        def fetch(b):
            entries = slice(b * BLK // LANES, (b + 1) * BLK // LANES)
            corners = {}
            for part, (engine, tag, members) in enumerate(fetch_plan[b]):
                home = sbuf_tile([P, len(members), BLK], F32, "corners%d_%d" % (b, part), tag)
                for place, (t, n) in enumerate(members):
                    window = y[t][:].indirect(corner_lists[n][:, entries])
                    if engine == "scalar":
                        nc.scalar.activation(home[:, place], window, ACT.Copy, scale=CORNER_SIGNS[n])
                    elif CORNER_SIGNS[n] > 0:
                        nc.vector.tensor_copy(home[:, place], window)
                    else:
                        nc.vector.tensor_scalar(home[:, place], window, CORNER_SIGNS[n], 0.0, ALU.mult, ALU.add)
                    corners[t, n] = home[:, place]
                if part == 0:
                    first_corner[b] = home[:, 0:PACK]
            differences[b] = [bank_tile([P, PACK, P], "diff%d_%d" % (b, n), DIFF_BANKS[b % 2][n]) for n in range(3)]
            for t in range(PACK):
                for bank, (first, second) in zip(differences[b], DIFFERENCES):
                    turn(bank[:, t, :], corners[t, first], True, False)
                    turn(bank[:, t, :], corners[t, second], False, True)

        x_two = (pick_words("x_two", two_sb, "w1_stage1"), scale_two)
        w2_q = quantize_weight("w2", w2_raw, True)
        fetch(0)
        x_thr = (pick_words("x_thr", thr_sb, "w2_stage1"), scale_thr)
        w3_q = quantize_weight("w3", w3_raw, True)
        w4_q = quantize_weight("w4", w4_raw, False)

        def fraction(name, x_picked, w_q, b, count):
            bank = bank_tile([P, PACK, P], "%s_bank%d" % (name, b), FRACTION_BANKS[count % len(FRACTION_BANKS)])
            product(bank[:].rearrange("j t p -> j (t p)"), x_picked, slice(b * BLK, (b + 1) * BLK), w_q, slice(0, H))
            frac = sbuf_tile([P, PACK, P], F32, "%s%d" % (name, b))
            nc.scalar.activation(frac[:], bank[:], ACT.Sigmoid)
            return frac

        fractions = [(fraction("fx", x_two, w2_q, b, 2 * b), fraction("fy", x_thr, w3_q, b, 2 * b + 1)) for b in range(NBLK)]

        def weigh(b):
            fx, fy = fractions[b]
            a_b, a_c, d_c = differences[b]
            f_dc = sbuf_tile([P, PACK, P], F32, "f_dc%d" % b, "w4_stage1" if b == 0 else None)
            nc.vector.tensor_tensor(f_dc[:], fx[:], fy[:], ALU.mult)
            f_ab = sbuf_tile([P, PACK, P], F32, "f_ab%d" % b, "w4_stage0" if b == 0 else None)
            nc.vector.scalar_tensor_tensor(f_ab[:], fy[:], 1.0, fx[:], ALU.subtract, ALU.mult)
            terms[b] = [sbuf_tile([P, PACK, P], F32, "term%d_%d" % (b, n)) for n in range(3)]
            nc.vector.tensor_tensor(terms[b][0][:], a_b[:], f_ab[:], ALU.mult)
            nc.vector.scalar_tensor_tensor(terms[b][1][:], a_c[:], -1.0, fy[:], ALU.mult, ALU.mult)
            nc.vector.tensor_tensor(terms[b][2][:], d_c[:], f_dc[:], ALU.mult)

        def finish(b):
            back = bank_tile([P, PACK, BLK], "back%d" % b, LAST_BACK_BANK if b == NBLK - 1 else BACK_BANK)
            for n, term in enumerate(terms[b]):
                for t in range(PACK):
                    turn(back[:, t, :], term[:, t, :], n == 0 and t == 0, n == len(terms[b]) - 1 and t == PACK - 1)
            z = sbuf_tile([P, BLK * PACK], BF16, "z%d" % b)
            nc.vector.tensor_tensor(
                z[:].rearrange("p (c i t) -> p c t i", i=2, t=PACK),
                back[:].rearrange("p t (c i) -> p c t i", i=2),
                first_corner[b].rearrange("p t (c i) -> p c t i", i=2),
                ALU.add,
            )
            z_q[b] = quantize("z%d" % b, z)

        out_rows = out.rearrange("(g p) j -> p g j", p=P)
        groups = N // P

        def project(b):
            if b == NBLK - 1:
                parts = ((0, groups // 2, LAST_OUT_BANKS[0], nc.scalar.copy), (groups // 2, groups // 2, LAST_OUT_BANKS[1], nc.vector.tensor_copy))
            else:
                parts = ((0, groups, OUT_BANK, nc.scalar.copy),)
            for g0, width, bank_number, copy in parts:
                acc = bank_tile([P, width, BLK], "acc%d_%d" % (b, g0), bank_number)
                for g in range(width):
                    product(acc[:, g, :], w4_q, slice((g0 + g) * P, (g0 + g + 1) * P), z_q[b], slice(0, BLK))
                result = keep.tile([P, width, BLK], F32, name="result%d_%d" % (b, g0))
                copy(result[:], acc[:])
                nc.sync.dma_start(out_rows[:, g0 : g0 + width, b * BLK : (b + 1) * BLK], result[:])

        for b in range(NBLK):
            if b + 1 < NBLK:
                fetch(b + 1)
            weigh(b)
            finish(b)
            if b > 0:
                project(b - 1)
        project(NBLK - 1)
